import numpy as np, ml_dtypes
CORES = [0,1]
N = 2
def setup_inputs(rng):
    return {"x": rng.standard_normal((N, 128, 8), dtype=np.float32).astype(ml_dtypes.bfloat16)}
def reference(x):
    s = x.min(axis=0)
    return {"y": np.broadcast_to(s, (N,) + s.shape)}

@@ -1,0 +1,38 @@
+from concourse.bass import DstId, RemoteDMATransfer
+
+SCRATCH = {
+    "mine": ("sbuf", [128, 8], "bfloat16"),
+    "land": ("sbuf", [128, 8], "bfloat16"),
+    "res": ("sbuf", [128, 8], "bfloat16"),
+}
+SEMAPHORES = ["loaded", "arrived", "folded", "sent", "stored"]
+
+ALU_MIN = 3
+
+
+def rank_program(g, core, T, topo):
+    rank = T.rank_of(core)
+    if rank is None:
+        return
+    peer = T.cores[1 - rank]
+    rid, pid, _se = topo.addr(peer)
+    mask = topo.mask(core, peer)
+    neng = bin(mask).count("1")
+
+    g.sync.dma_start(T.mine[:], T.x[:]).then_inc(T.sem.loaded, 16)
+    g.wait_ge(T.sem.loaded, 16)
+
+    g.remote_dma(T.land[:], T.mine[:], remote_sem=T.sem.arrived, local_sem=T.sem.sent,
+                 pid=pid, routing_id=rid, dma_engine_mask=mask)
+
+    g.wait_ge(T.sem.arrived, neng)
+    g.remote_dma_fused(
+        [RemoteDMATransfer(dst_ids=[DstId(rid=rid, pnc=pid)], dma_engine_mask=mask, remote_sem=T.sem.folded,
+                           srcs=[T.mine[:], T.land[:]], dsts=[T.res[:]], alu_op=ALU_MIN)],
+        local_sem=T.sem.sent)
+
+    g.sync.wait_ge(T.sem.folded, neng)
+    g.sync.dma_start(T.y[:], T.res[:]).then_inc(T.sem.stored, 16)
+    g.sync.wait_ge(T.sem.stored, 16)
+
+    g.wait_ge(T.sem.sent, 2 * neng)

@@ -1,9 +1,9 @@
 from concourse.bass import DstId, RemoteDMATransfer
 
 SCRATCH = {
-    "mine": ("sbuf", [128, 8], "bfloat16"),
-    "land": ("sbuf", [128, 8], "bfloat16"),
-    "res": ("sbuf", [128, 8], "bfloat16"),
+    "mine": ("dram", [128, 8], "bfloat16"),
+    "land": ("dram", [128, 8], "bfloat16"),
+    "res": ("dram", [128, 8], "bfloat16"),
 }
 SEMAPHORES = ["loaded", "arrived", "folded", "sent", "stored"]
 

from concourse.bass import DstId, RemoteDMATransfer

SCRATCH = {
    "mine": ("dram", [128, 8], "bfloat16"),
    "land": ("dram", [128, 8], "bfloat16"),
    "res": ("dram", [128, 8], "bfloat16"),
}
SEMAPHORES = ["loaded", "arrived", "folded", "sent", "stored"]

ALU_MIN = 3


def rank_program(g, core, T, topo):
    rank = T.rank_of(core)
    if rank is None:
        return
    peer = T.cores[1 - rank]
    rid, pid, _se = topo.addr(peer)
    mask = topo.mask(core, peer)
    neng = bin(mask).count("1")

    g.sync.dma_start(T.mine[:], T.x[:]).then_inc(T.sem.loaded, 16)
    g.wait_ge(T.sem.loaded, 16)

    g.remote_dma(T.land[:], T.mine[:], remote_sem=T.sem.arrived, local_sem=T.sem.sent,
                 pid=pid, routing_id=rid, dma_engine_mask=mask)

    g.wait_ge(T.sem.arrived, neng)
    g.remote_dma_fused(
        [RemoteDMATransfer(dst_ids=[DstId(rid=rid, pnc=pid)], dma_engine_mask=mask, remote_sem=T.sem.folded,
                           srcs=[T.mine[:], T.land[:]], dsts=[T.res[:]], alu_op=ALU_MIN)],
        local_sem=T.sem.sent)

    g.sync.wait_ge(T.sem.folded, neng)
    g.sync.dma_start(T.y[:], T.res[:]).then_inc(T.sem.stored, 16)
    g.sync.wait_ge(T.sem.stored, 16)

    g.wait_ge(T.sem.sent, 2 * neng)
